import numpy as np
import ml_dtypes


def mxq(x, axis, fmt="e4m3"):
    dtype, down = {"e4m3": (ml_dtypes.float8_e4m3fn, 7), "e5m2": (ml_dtypes.float8_e5m2, 14)}[fmt]
    v = np.moveaxis(np.asarray(x, np.float32).astype(ml_dtypes.bfloat16).astype(np.float64), axis, -1)
    blocks = v.reshape(v.shape[:-1] + (-1, 32))
    amax = np.abs(blocks).max(-1, keepdims=True)
    byte = np.maximum(np.where(amax > 0, np.frexp(amax)[1] - 1 + 127, 0) - down, 1)
    scale = np.exp2(byte - 127.0)
    codes = (blocks / scale).astype(np.float32).astype(dtype).astype(np.float64)
    return np.moveaxis((codes * scale).reshape(v.shape), -1, axis)


WIDE = False


def mx_kscale(k):
    if not WIDE:
        return np.ones(k)
    levels = np.array([10, -10, 5, -5, 0])
    if k % 512:
        return np.exp2(np.random.permutation(np.resize(levels, k // 32))).repeat(32)
    a = np.empty((k // 512, 16))
    for p in range(k // 512):
        a[p, :8] = np.random.permutation(np.resize(levels, 8))
        for g in range(8):
            far = levels[np.abs(levels - a[p, g]) >= 10]
            a[p, g + 8] = far[np.random.randint(len(far))]
    return np.exp2(a.ravel()).repeat(32)


def f64(x):
    return np.asarray(x).astype(np.float64)


def striped8(idx):
    return np.asarray(idx).reshape(8, -1, 16).transpose(0, 2, 1).reshape(128, -1).astype(np.uint16)


def unstriped8(offs):
    return offs.reshape(8, 16, -1).transpose(0, 2, 1).reshape(8, -1).astype(np.int64)


def pick8(x, idx, run):
    r = np.arange(len(x))
    return x[r[:, None], idx[r % (8 * run) // run]]


E2M1 = np.array([0.0, 0.5, 1.0, 1.5, 2.0, 3.0, 4.0, 6.0, -0.0, -0.5, -1.0, -1.5, -2.0, -3.0, -4.0, -6.0])


def pack_weight(w, fmt):
    k, n = w.shape
    w = f64(np.asarray(w, np.float32).astype(ml_dtypes.bfloat16)).reshape(k // 32, 32, n)
    amax = np.abs(w).max(1)
    if fmt == "e4m3":
        byte = np.frexp(amax)[1] - 1 + 127 - 7
    else:
        mant, ex = np.frexp(amax / 6.0)
        byte = np.where(mant > 0.5, ex, ex - 1) + 127
    byte = np.clip(np.where(amax > 0, byte, 1), 1, 254)
    scaled = (w * np.exp2(127.0 - byte)[:, None, :]).reshape(k, n).astype(np.float32)
    by_word = np.ascontiguousarray(scaled.reshape(k // 512, 128, 4, n).transpose(0, 1, 3, 2))
    if fmt == "e4m3":
        words = by_word.astype(ml_dtypes.float8_e4m3fn).view(np.uint8)
    else:
        c = by_word.astype(ml_dtypes.float4_e2m1fn).view(np.uint8) & 0xF
        words = (c[..., 0::2] | (c[..., 1::2] << 4)).reshape(k // 512, 128, 2 * n)
    return np.ascontiguousarray(words), np.ascontiguousarray(byte.astype(np.uint8).reshape(k // 512, 16, n))


def unpack_weight(words, scales, fmt):
    g, _, n = scales.shape
    words = np.ascontiguousarray(words).reshape(g, 128, n, -1)
    if fmt == "e4m3":
        vals = words.view(ml_dtypes.float8_e4m3fn).astype(np.float64)
    else:
        nib = np.empty((g, 128, n, 4), np.uint8)
        nib[..., 0::2] = words & 0xF
        nib[..., 1::2] = words >> 4
        vals = E2M1[nib]
    vals = vals * np.repeat(np.exp2(scales.astype(np.float64) - 127.0), 8, axis=1)[..., None]
    return vals.transpose(0, 1, 3, 2).reshape(g * 512, n)


D, T, I, Q = 512, 1024, 512, 128


def setup_inputs():
    n = np.random.standard_normal
    idx = np.stack([np.random.permutation(T)[:I] for _ in range(8)])
    idx2 = np.stack([np.random.permutation(T)[:I] for _ in range(8)])
    fd = mx_kscale(D)
    keysp = pack_weight(n((D, T)) / fd[:, None], "e2m1")
    return {
        "query": (n((D, Q)) * 0.9 / np.sqrt(D) * fd[:, None]).astype(np.float32),
        "query2": (n((D, Q)) * 0.9 / np.sqrt(D) * fd[:, None]).astype(np.float32),
        "keys_words": keysp[0],
        "keys_scales": keysp[1],
        "lam": (np.random.uniform(0.5, 1.3, (Q, 1))).astype(np.float32),
        "width": (np.random.uniform(0.3, 0.8, (Q, 1))).astype(np.float32),
        "old": (np.random.uniform(0.0, 2.0, (Q, T))).astype(np.float32),
        "fade": (np.random.uniform(0.3, 0.9, (Q, 1))).astype(np.float32),
        "offs": striped8(idx),
        "offs2": striped8(idx2),
    }


def reference(query, query2, keys_words, keys_scales, lam, width, old, fade, offs, offs2):
    idx = unstriped8(offs)
    idx2 = unstriped8(offs2)
    keysu = unpack_weight(keys_words, keys_scales, "e2m1")
    queryq = mxq(f64(query), 0, "e4m3")
    a = queryq.T @ keysu
    query2q = mxq(f64(query2), 0, "e4m3")
    b = query2q.T @ keysu
    s = (np.maximum(pick8(a, idx, 16), pick8(b, idx2, 16)) - np.maximum(pick8(a, idx2, 16), pick8(b, idx, 16))) * f64(lam)
    ce = (s - np.mean(s, axis=1, keepdims=True)) / f64(width)
    p = 1.0 / (np.square(ce) + 1.0)
    w = p / np.sum(p, axis=1, keepdims=True)
    ws = w * 512.0
    wf = np.zeros((Q, T))
    wf[np.arange(Q)[:, None], idx[np.arange(Q) % 128 // 16]] = ws
    y = f64(old) * f64(fade) + wf
    return y

@@ -1,0 +1,159 @@
+from contextlib import ExitStack
+
+import concourse.mybir as mybir
+
+D, T, I, Q = 512, 1024, 512, 128
+FLOPS = 2 * 2 * D * T * Q
+
+F32 = mybir.dt.float32
+BF16 = mybir.dt.bfloat16
+I32 = mybir.dt.int32
+U32 = mybir.dt.uint32
+U16 = mybir.dt.uint16
+U8 = mybir.dt.uint8
+FP8X4 = mybir.dt.float8_e4m3fn_x4
+FP4X4 = mybir.dt.float4_e2m1fn_x4
+ALU = mybir.AluOpType
+ACT = mybir.ActivationFunctionType
+
+P = 128
+PACK = 4
+N_PASS = 256
+HALF = I // 2
+OUT_EDGES = (0, 384, 704, 896, 1024)
+
+
+def tile_attend_exchanged_typical_counts_heads_kernel(
+    tc, query, query2, keys_words, keys_scales, lam, width, old, fade, offs, offs2, out
+):
+    nc = tc.nc
+    with ExitStack() as ctx:
+        lists = ctx.enter_context(tc.tile_pool(name="lists", bufs=1))
+        sb = ctx.enter_context(tc.tile_pool(name="sb", bufs=1))
+        psum = ctx.enter_context(tc.psum_pool(name="psum", bufs=1))
+
+        key_scale = sb.tile([P, T], U8, name="key_scale", align_bytes=64)
+        nc.gpsimd.memset(key_scale[:].bitcast(I32), 0)
+
+        raw_a = sb.tile([P, PACK, Q], F32, name="raw_a", tag="stage")
+        nc.sync.dma_start(out=raw_a[:], in_=query.rearrange("(p j) q -> p j q", j=PACK))
+        key_words = sb.tile([P, 2 * T], U8, name="key_words", align_bytes=64)
+        nc.sync.dma_start(out=key_words[:].bitcast(I32), in_=keys_words[0].bitcast(I32))
+        for quad in range(4):
+            nc.sync.dma_start(
+                out=key_scale[32 * quad : 32 * quad + 4, :].bitcast(I32),
+                in_=keys_scales[0, 4 * quad : 4 * quad + 4, :].bitcast(I32),
+            )
+        raw_b = sb.tile([P, PACK, Q], F32, name="raw_b")
+        nc.sync.dma_start(out=raw_b[:], in_=query2.rearrange("(p j) q -> p j q", j=PACK))
+
+        width_col = sb.tile([P, 1], F32, name="width_col")
+        nc.scalar.dma_start(out=width_col[:], in_=width)
+        lam_col = sb.tile([P, 1], F32, name="lam_col")
+        nc.gpsimd.dma_start(out=lam_col[:], in_=lam)
+        fade_col = sb.tile([P, 1], F32, name="fade_col")
+        nc.gpsimd.dma_start(out=fade_col[:], in_=fade)
+
+        list1 = lists.tile([P, I // 16], U16, name="list1")
+        nc.sync.dma_start(list1[:], offs)
+        list2 = lists.tile([P, I // 16], U16, name="list2")
+        nc.sync.dma_start(list2[:], offs2)
+
+        placed = sb.tile([P, T], F32, name="placed")
+        nc.gpsimd.memset(placed[:], 0.0)
+
+        root_w = sb.tile([P, 1], F32, name="root_w")
+        nc.scalar.activation(root_w[:], width_col[:], ACT.Abs_reciprocal_sqrt)
+
+        scores = []
+        for name, raw in (("a", raw_a), ("b", raw_b)):
+            grouped = sb.tile([P, Q, PACK], BF16, name="grouped_" + name, align_bytes=64)
+            nc.vector.tensor_copy(out=grouped[:], in_=raw[:].rearrange("p j q -> p q j"))
+            codes = sb.tile([P, Q], U32, name="codes_" + name, align_bytes=64)
+            scale = sb.tile([P, Q], U8, name="scale_" + name, align_bytes=64)
+            nc.vector.quantize_mx(
+                out=codes[:].bitcast(FP8X4),
+                scales=scale[:],
+                in_=grouped[:].rearrange("p q j -> p (q j)"),
+            )
+            whole = sb.tile([P, T], F32, name="whole_" + name)
+            for n0 in range(0, T, N_PASS):
+                bank = psum.tile([P, N_PASS], F32, name="bank_%s%d" % (name, n0))
+                nc.tensor.matmul_mx(
+                    out=bank[:],
+                    lhsT=codes[:].bitcast(FP8X4),
+                    lhsT_scale=scale[:],
+                    rhs=key_words[:, 2 * n0 : 2 * (n0 + N_PASS)].bitcast(FP4X4),
+                    rhs_scale=key_scale[:, n0 : n0 + N_PASS],
+                    start=True,
+                    stop=True,
+                )
+                nc.scalar.activation(whole[:, n0 : n0 + N_PASS], bank[:], ACT.Copy)
+            scores.append(whole)
+        a_all, b_all = scores
+
+        old_rows = sb.tile([P, T], F32, name="old_rows", tag="stage")
+        nc.sync.dma_start(out=old_rows[:], in_=old)
+
+        slope = sb.tile([P, 1], F32, name="slope")
+        nc.vector.scalar_tensor_tensor(slope[:], root_w[:], lam_col[:], root_w[:], ALU.mult, ALU.mult)
+        mean_factor = sb.tile([P, 1], F32, name="mean_factor")
+        nc.vector.tensor_scalar(mean_factor[:], slope[:], 1.0 / I, None, ALU.mult)
+
+        halves = [slice(0, HALF), slice(HALF, I)]
+        cols = [slice(0, HALF // 16), slice(HALF // 16, I // 16)]
+        a1 = sb.tile([P, I], F32, name="a1")
+        a2 = sb.tile([P, I], F32, name="a2")
+        b2 = sb.tile([P, I], F32, name="b2")
+        nc.vector.tensor_copy(a1[:], a_all[:].indirect(list1[:]))
+        nc.vector.tensor_copy(a2[:], a_all[:].indirect(list2[:]))
+        nc.scalar.activation(b2[:], b_all[:].indirect(list2[:]), ACT.Copy)
+        b1 = [sb.tile([P, HALF], F32, name="b1_%d" % h) for h in range(2)]
+        for h in range(2):
+            nc.scalar.activation(b1[h][:], b_all[:].indirect(list1[:, cols[h]]), ACT.Copy)
+
+        first = sb.tile([P, I], F32, name="first")
+        sum_first = sb.tile([P, 1], F32, name="sum_first")
+        nc.vector.scalar_tensor_tensor(first[:], a1[:], 1.0, b2[:], ALU.mult, ALU.max, accum_out=sum_first[:])
+        second = [sb.tile([P, HALF], F32, name="second_%d" % h) for h in range(2)]
+        sum_second = [sb.tile([P, 1], F32, name="sum_second_%d" % h) for h in range(2)]
+        diff = [sb.tile([P, HALF], F32, name="diff_%d" % h) for h in range(2)]
+        nc.vector.scalar_tensor_tensor(
+            second[0][:], a2[:, halves[0]], 1.0, b1[0][:], ALU.mult, ALU.max, accum_out=sum_second[0][:]
+        )
+        nc.vector.tensor_tensor(diff[0][:], first[:, halves[0]], second[0][:], ALU.subtract)
+        rest = sb.tile([P, 1], F32, name="rest")
+        nc.vector.tensor_tensor(rest[:], sum_first[:], sum_second[0][:], ALU.subtract)
+        nc.vector.scalar_tensor_tensor(
+            second[1][:], a2[:, halves[1]], 1.0, b1[1][:], ALU.mult, ALU.max, accum_out=sum_second[1][:]
+        )
+        shift = sb.tile([P, 1], F32, name="shift")
+        nc.vector.tensor_scalar(shift[:], sum_second[1][:], rest[:], mean_factor[:], ALU.subtract, ALU.mult)
+        nc.vector.tensor_tensor(diff[1][:], first[:, halves[1]], second[1][:], ALU.subtract)
+
+        sq = [sb.tile([P, HALF], F32, name="sq_%d" % h) for h in range(2)]
+        for h in range(2):
+            nc.scalar.activation(sq[h][:], diff[h][:], ACT.Square, bias=shift[:], scale=slope[:])
+        root = sb.tile([P, I], F32, name="root")
+        for h in range(2):
+            nc.scalar.activation(root[:, halves[h]], sq[h][:], ACT.Abs_reciprocal_sqrt, bias=1.0)
+
+        part = sb.tile([P, I], F32, name="part")
+        total = sb.tile([P, 1], F32, name="total")
+        nc.vector.scalar_tensor_tensor(
+            part[:], root[:], 1.0 / 512.0, root[:], ALU.mult, ALU.mult, accum_out=total[:]
+        )
+        inv_total = sb.tile([P, 1], F32, name="inv_total")
+        nc.vector.reciprocal(inv_total[:], total[:])
+        ws = sb.tile([P, I], F32, name="ws")
+        nc.vector.tensor_scalar(ws[:], part[:], inv_total[:], 512.0, ALU.mult, ALU.mult)
+        nc.vector.tensor_copy(placed[:].indirect(list1[:]), ws[:])
+
+        for c in range(len(OUT_EDGES) - 1):
+            span = slice(OUT_EDGES[c], OUT_EDGES[c + 1])
+            result = sb.tile([P, span.stop - span.start], F32, name="result_%d" % c)
+            nc.vector.scalar_tensor_tensor(
+                result[:], old_rows[:, span], fade_col[:], placed[:, span], ALU.mult, ALU.add
+            )
+            queue = nc.sync if c % 2 == 0 else nc.scalar
+            queue.dma_start(out=out[:, span], in_=result[:])

@@ -20,7 +20,7 @@ P = 128
 PACK = 4
 N_PASS = 256
 HALF = I // 2
-OUT_EDGES = (0, 384, 704, 896, 1024)
+OUT_EDGES = (0, 128, 384, 640, 896, 1024)
 
 
 def tile_attend_exchanged_typical_counts_heads_kernel(
@@ -37,45 +37,52 @@ def tile_attend_exchanged_typical_counts_heads_kernel(
 
         raw_a = sb.tile([P, PACK, Q], F32, name="raw_a", tag="stage")
         nc.sync.dma_start(out=raw_a[:], in_=query.rearrange("(p j) q -> p j q", j=PACK))
-        key_words = sb.tile([P, 2 * T], U8, name="key_words", align_bytes=64)
-        nc.sync.dma_start(out=key_words[:].bitcast(I32), in_=keys_words[0].bitcast(I32))
         for quad in range(4):
             nc.sync.dma_start(
                 out=key_scale[32 * quad : 32 * quad + 4, :].bitcast(I32),
                 in_=keys_scales[0, 4 * quad : 4 * quad + 4, :].bitcast(I32),
             )
+        key_words = sb.tile([P, 2 * T], U8, name="key_words", align_bytes=64)
+        nc.sync.dma_start(out=key_words[:].bitcast(I32), in_=keys_words[0].bitcast(I32))
         raw_b = sb.tile([P, PACK, Q], F32, name="raw_b")
         nc.sync.dma_start(out=raw_b[:], in_=query2.rearrange("(p j) q -> p j q", j=PACK))
-
-        width_col = sb.tile([P, 1], F32, name="width_col")
-        nc.scalar.dma_start(out=width_col[:], in_=width)
-        lam_col = sb.tile([P, 1], F32, name="lam_col")
-        nc.gpsimd.dma_start(out=lam_col[:], in_=lam)
-        fade_col = sb.tile([P, 1], F32, name="fade_col")
-        nc.gpsimd.dma_start(out=fade_col[:], in_=fade)
 
         list1 = lists.tile([P, I // 16], U16, name="list1")
         nc.sync.dma_start(list1[:], offs)
         list2 = lists.tile([P, I // 16], U16, name="list2")
         nc.sync.dma_start(list2[:], offs2)
 
-        placed = sb.tile([P, T], F32, name="placed")
-        nc.gpsimd.memset(placed[:], 0.0)
+        width_col = sb.tile([P, 1], F32, name="width_col")
+        nc.sync.dma_start(out=width_col[:], in_=width)
+        lam_col = sb.tile([P, 1], F32, name="lam_col")
+        nc.sync.dma_start(out=lam_col[:], in_=lam)
+        fade_col = sb.tile([P, 1], F32, name="fade_col")
+        nc.sync.dma_start(out=fade_col[:], in_=fade)
 
-        root_w = sb.tile([P, 1], F32, name="root_w")
-        nc.scalar.activation(root_w[:], width_col[:], ACT.Abs_reciprocal_sqrt)
+        placed = sb.tile([P, T], F32, name="placed")
+        nc.vector.memset(placed[:], 0.0)
+
+        count = sb.tile([P, 1], F32, name="count")
+        nc.vector.memset(count[:], 512.0)
+        root_count = sb.tile([P, 1], F32, name="root_count")
+        nc.scalar.activation(root_count[:], count[:], ACT.Abs_reciprocal_sqrt)
 
         scores = []
         for name, raw in (("a", raw_a), ("b", raw_b)):
-            grouped = sb.tile([P, Q, PACK], BF16, name="grouped_" + name, align_bytes=64)
-            nc.vector.tensor_copy(out=grouped[:], in_=raw[:].rearrange("p j q -> p q j"))
+            grouped = [
+                sb.tile([P, Q // 2, PACK], BF16, name="grouped_%s%d" % (name, h), align_bytes=64) for h in range(2)
+            ]
             codes = sb.tile([P, Q], U32, name="codes_" + name, align_bytes=64)
             scale = sb.tile([P, Q], U8, name="scale_" + name, align_bytes=64)
-            nc.vector.quantize_mx(
-                out=codes[:].bitcast(FP8X4),
-                scales=scale[:],
-                in_=grouped[:].rearrange("p q j -> p (q j)"),
-            )
+            rows = [slice(0, Q // 2), slice(Q // 2, Q)]
+            for h in range(2):
+                nc.vector.tensor_copy(out=grouped[h][:], in_=raw[:, :, rows[h]].rearrange("p j q -> p q j"))
+            for h in range(2):
+                nc.vector.quantize_mx(
+                    out=codes[:, rows[h]].bitcast(FP8X4),
+                    scales=scale[:, rows[h]],
+                    in_=grouped[h][:].rearrange("p q j -> p (q j)"),
+                )
             whole = sb.tile([P, T], F32, name="whole_" + name)
             for n0 in range(0, T, N_PASS):
                 bank = psum.tile([P, N_PASS], F32, name="bank_%s%d" % (name, n0))
@@ -95,58 +102,70 @@ def tile_attend_exchanged_typical_counts_heads_kernel(
         old_rows = sb.tile([P, T], F32, name="old_rows", tag="stage")
         nc.sync.dma_start(out=old_rows[:], in_=old)
 
-        slope = sb.tile([P, 1], F32, name="slope")
-        nc.vector.scalar_tensor_tensor(slope[:], root_w[:], lam_col[:], root_w[:], ALU.mult, ALU.mult)
-        mean_factor = sb.tile([P, 1], F32, name="mean_factor")
-        nc.vector.tensor_scalar(mean_factor[:], slope[:], 1.0 / I, None, ALU.mult)
+        minus_one = sb.tile([P, 1], F32, name="minus_one")
+        nc.gpsimd.memset(minus_one[:], -1.0)
+        wide_sq = sb.tile([P, 1], F32, name="wide_sq")
+        nc.gpsimd.tensor_scalar(wide_sq[:], width_col[:], width_col[:], float(I * I), ALU.mult, ALU.mult)
+        inv_wide_sq = sb.tile([P, 1], F32, name="inv_wide_sq")
+        nc.gpsimd.tensor_tensor(inv_wide_sq[:], wide_sq[:], minus_one[:], ALU.pow)
+        steep = sb.tile([P, 1], F32, name="steep")
+        nc.gpsimd.tensor_scalar(steep[:], inv_wide_sq[:], lam_col[:], lam_col[:], ALU.mult, ALU.mult)
 
         halves = [slice(0, HALF), slice(HALF, I)]
         cols = [slice(0, HALF // 16), slice(HALF // 16, I // 16)]
         a1 = sb.tile([P, I], F32, name="a1")
         a2 = sb.tile([P, I], F32, name="a2")
-        b2 = sb.tile([P, I], F32, name="b2")
         nc.vector.tensor_copy(a1[:], a_all[:].indirect(list1[:]))
         nc.vector.tensor_copy(a2[:], a_all[:].indirect(list2[:]))
-        nc.scalar.activation(b2[:], b_all[:].indirect(list2[:]), ACT.Copy)
         b1 = [sb.tile([P, HALF], F32, name="b1_%d" % h) for h in range(2)]
+        b2 = [sb.tile([P, HALF], F32, name="b2_%d" % h) for h in range(2)]
         for h in range(2):
+            nc.scalar.activation(b2[h][:], b_all[:].indirect(list2[:, cols[h]]), ACT.Copy)
             nc.scalar.activation(b1[h][:], b_all[:].indirect(list1[:, cols[h]]), ACT.Copy)
 
-        first = sb.tile([P, I], F32, name="first")
-        sum_first = sb.tile([P, 1], F32, name="sum_first")
-        nc.vector.scalar_tensor_tensor(first[:], a1[:], 1.0, b2[:], ALU.mult, ALU.max, accum_out=sum_first[:])
+        first = [sb.tile([P, HALF], F32, name="first_%d" % h) for h in range(2)]
         second = [sb.tile([P, HALF], F32, name="second_%d" % h) for h in range(2)]
-        sum_second = [sb.tile([P, 1], F32, name="sum_second_%d" % h) for h in range(2)]
         diff = [sb.tile([P, HALF], F32, name="diff_%d" % h) for h in range(2)]
+        sum_diff0 = sb.tile([P, 1], F32, name="sum_diff0")
+        sum_first1 = sb.tile([P, 1], F32, name="sum_first1")
+        sum_second1 = sb.tile([P, 1], F32, name="sum_second1")
+        nc.vector.tensor_tensor(first[0][:], a1[:, halves[0]], b2[0][:], ALU.max)
+        nc.vector.tensor_tensor(second[0][:], a2[:, halves[0]], b1[0][:], ALU.max)
         nc.vector.scalar_tensor_tensor(
-            second[0][:], a2[:, halves[0]], 1.0, b1[0][:], ALU.mult, ALU.max, accum_out=sum_second[0][:]
+            first[1][:], a1[:, halves[1]], 1.0, b2[1][:], ALU.mult, ALU.max, accum_out=sum_first1[:]
         )
-        nc.vector.tensor_tensor(diff[0][:], first[:, halves[0]], second[0][:], ALU.subtract)
-        rest = sb.tile([P, 1], F32, name="rest")
-        nc.vector.tensor_tensor(rest[:], sum_first[:], sum_second[0][:], ALU.subtract)
         nc.vector.scalar_tensor_tensor(
-            second[1][:], a2[:, halves[1]], 1.0, b1[1][:], ALU.mult, ALU.max, accum_out=sum_second[1][:]
+            diff[0][:], first[0][:], 1.0, second[0][:], ALU.mult, ALU.subtract, accum_out=sum_diff0[:]
         )
-        shift = sb.tile([P, 1], F32, name="shift")
-        nc.vector.tensor_scalar(shift[:], sum_second[1][:], rest[:], mean_factor[:], ALU.subtract, ALU.mult)
-        nc.vector.tensor_tensor(diff[1][:], first[:, halves[1]], second[1][:], ALU.subtract)
+        nc.vector.scalar_tensor_tensor(
+            second[1][:], a2[:, halves[1]], 1.0, b1[1][:], ALU.mult, ALU.max, accum_out=sum_second1[:]
+        )
+        minus_sum = sb.tile([P, 1], F32, name="minus_sum")
+        nc.vector.tensor_scalar(
+            minus_sum[:], sum_second1[:], sum_diff0[:], sum_first1[:], ALU.subtract, ALU.subtract
+        )
+        nc.vector.tensor_tensor(diff[1][:], first[1][:], second[1][:], ALU.subtract)
 
         sq = [sb.tile([P, HALF], F32, name="sq_%d" % h) for h in range(2)]
         for h in range(2):
-            nc.scalar.activation(sq[h][:], diff[h][:], ACT.Square, bias=shift[:], scale=slope[:])
-        root = sb.tile([P, I], F32, name="root")
+            nc.scalar.activation(sq[h][:], diff[h][:], ACT.Square, bias=minus_sum[:], scale=float(I))
+        root = [sb.tile([P, HALF], F32, name="root_%d" % h) for h in range(2)]
         for h in range(2):
-            nc.scalar.activation(root[:, halves[h]], sq[h][:], ACT.Abs_reciprocal_sqrt, bias=1.0)
+            nc.scalar.activation(root[h][:], sq[h][:], ACT.Abs_reciprocal_sqrt, bias=1.0, scale=steep[:])
 
-        part = sb.tile([P, I], F32, name="part")
-        total = sb.tile([P, 1], F32, name="total")
+        part0 = sb.tile([P, HALF], F32, name="part0")
+        total0 = sb.tile([P, 1], F32, name="total0")
         nc.vector.scalar_tensor_tensor(
-            part[:], root[:], 1.0 / 512.0, root[:], ALU.mult, ALU.mult, accum_out=total[:]
+            part0[:], root[0][:], 1.0, root[0][:], ALU.mult, ALU.mult, accum_out=total0[:]
         )
-        inv_total = sb.tile([P, 1], F32, name="inv_total")
-        nc.vector.reciprocal(inv_total[:], total[:])
+        part1 = sb.tile([P, HALF], F32, name="part1")
+        total1 = sb.tile([P, 1], F32, name="total1")
+        nc.scalar.activation(part1[:], root[1][:], ACT.Square, scale=root_count[:], accum_out=total1[:])
+        gain = sb.tile([P, 1], F32, name="gain")
+        nc.scalar.activation(gain[:], total0[:], ACT.Abs_reciprocal_sqrt, bias=total1[:], scale=1.0 / 512.0)
         ws = sb.tile([P, I], F32, name="ws")
-        nc.vector.tensor_scalar(ws[:], part[:], inv_total[:], 512.0, ALU.mult, ALU.mult)
+        nc.vector.tensor_scalar(ws[:, halves[0]], part0[:], gain[:], gain[:], ALU.mult, ALU.mult)
+        nc.scalar.activation(ws[:, halves[1]], root[1][:], ACT.Square, scale=gain[:])
         nc.vector.tensor_copy(placed[:].indirect(list1[:]), ws[:])
 
         for c in range(len(OUT_EDGES) - 1):

@@ -20,6 +20,7 @@ P = 128
 PACK = 4
 N_PASS = 256
 HALF = I // 2
+SPLIT = 320
 OUT_EDGES = (0, 128, 384, 640, 896, 1024)
 
 
@@ -83,7 +84,7 @@ def tile_attend_exchanged_typical_counts_heads_kernel(
                     scales=scale[:, rows[h]],
                     in_=grouped[h][:].rearrange("p q j -> p (q j)"),
                 )
-            whole = sb.tile([P, T], F32, name="whole_" + name)
+            whole = sb.tile([P, T], F32, name="whole_" + name, tag="whole_" + name)
             for n0 in range(0, T, N_PASS):
                 bank = psum.tile([P, N_PASS], F32, name="bank_%s%d" % (name, n0))
                 nc.tensor.matmul_mx(
@@ -102,15 +103,6 @@ def tile_attend_exchanged_typical_counts_heads_kernel(
         old_rows = sb.tile([P, T], F32, name="old_rows", tag="stage")
         nc.sync.dma_start(out=old_rows[:], in_=old)
 
-        minus_one = sb.tile([P, 1], F32, name="minus_one")
-        nc.gpsimd.memset(minus_one[:], -1.0)
-        wide_sq = sb.tile([P, 1], F32, name="wide_sq")
-        nc.gpsimd.tensor_scalar(wide_sq[:], width_col[:], width_col[:], float(I * I), ALU.mult, ALU.mult)
-        inv_wide_sq = sb.tile([P, 1], F32, name="inv_wide_sq")
-        nc.gpsimd.tensor_tensor(inv_wide_sq[:], wide_sq[:], minus_one[:], ALU.pow)
-        steep = sb.tile([P, 1], F32, name="steep")
-        nc.gpsimd.tensor_scalar(steep[:], inv_wide_sq[:], lam_col[:], lam_col[:], ALU.mult, ALU.mult)
-
         halves = [slice(0, HALF), slice(HALF, I)]
         cols = [slice(0, HALF // 16), slice(HALF // 16, I // 16)]
         a1 = sb.tile([P, I], F32, name="a1")
@@ -123,49 +115,60 @@ def tile_attend_exchanged_typical_counts_heads_kernel(
             nc.scalar.activation(b2[h][:], b_all[:].indirect(list2[:, cols[h]]), ACT.Copy)
             nc.scalar.activation(b1[h][:], b_all[:].indirect(list1[:, cols[h]]), ACT.Copy)
 
+        wide_sq = sb.tile([P, 1], F32, name="wide_sq", tag="whole_b")
+        nc.scalar.activation(wide_sq[:], width_col[:], ACT.Square, scale=float(I))
+        inv_wide = sb.tile([P, 1], F32, name="inv_wide")
+        nc.scalar.activation(inv_wide[:], wide_sq[:], ACT.Abs_reciprocal_sqrt)
+        steep = sb.tile([P, 1], F32, name="steep")
+        nc.scalar.activation(steep[:], inv_wide[:], ACT.Square, scale=lam_col[:])
+
         first = [sb.tile([P, HALF], F32, name="first_%d" % h) for h in range(2)]
         second = [sb.tile([P, HALF], F32, name="second_%d" % h) for h in range(2)]
         diff = [sb.tile([P, HALF], F32, name="diff_%d" % h) for h in range(2)]
+        sum_first = [sb.tile([P, 1], F32, name="sum_first_%d" % h) for h in range(2)]
+        sum_second = [sb.tile([P, 1], F32, name="sum_second_%d" % h) for h in range(2)]
         sum_diff0 = sb.tile([P, 1], F32, name="sum_diff0")
-        sum_first1 = sb.tile([P, 1], F32, name="sum_first1")
-        sum_second1 = sb.tile([P, 1], F32, name="sum_second1")
-        nc.vector.tensor_tensor(first[0][:], a1[:, halves[0]], b2[0][:], ALU.max)
-        nc.vector.tensor_tensor(second[0][:], a2[:, halves[0]], b1[0][:], ALU.max)
-        nc.vector.scalar_tensor_tensor(
-            first[1][:], a1[:, halves[1]], 1.0, b2[1][:], ALU.mult, ALU.max, accum_out=sum_first1[:]
-        )
-        nc.vector.scalar_tensor_tensor(
-            diff[0][:], first[0][:], 1.0, second[0][:], ALU.mult, ALU.subtract, accum_out=sum_diff0[:]
-        )
-        nc.vector.scalar_tensor_tensor(
-            second[1][:], a2[:, halves[1]], 1.0, b1[1][:], ALU.mult, ALU.max, accum_out=sum_second1[:]
-        )
+        for h in range(2):
+            nc.vector.scalar_tensor_tensor(
+                first[h][:], a1[:, halves[h]], 1.0, b2[h][:], ALU.mult, ALU.max, accum_out=sum_first[h][:]
+            )
+            if h == 1:
+                nc.vector.tensor_tensor(sum_diff0[:], sum_first[0][:], sum_second[0][:], ALU.subtract)
+            nc.vector.scalar_tensor_tensor(
+                second[h][:], a2[:, halves[h]], 1.0, b1[h][:], ALU.mult, ALU.max, accum_out=sum_second[h][:]
+            )
+        nc.vector.tensor_tensor(diff[0][:], first[0][:], second[0][:], ALU.subtract)
         minus_sum = sb.tile([P, 1], F32, name="minus_sum")
         nc.vector.tensor_scalar(
-            minus_sum[:], sum_second1[:], sum_diff0[:], sum_first1[:], ALU.subtract, ALU.subtract
+            minus_sum[:], sum_second[1][:], sum_diff0[:], sum_first[1][:], ALU.subtract, ALU.subtract
         )
         nc.vector.tensor_tensor(diff[1][:], first[1][:], second[1][:], ALU.subtract)
 
         sq = [sb.tile([P, HALF], F32, name="sq_%d" % h) for h in range(2)]
         for h in range(2):
             nc.scalar.activation(sq[h][:], diff[h][:], ACT.Square, bias=minus_sum[:], scale=float(I))
-        root = [sb.tile([P, HALF], F32, name="root_%d" % h) for h in range(2)]
-        for h in range(2):
-            nc.scalar.activation(root[h][:], sq[h][:], ACT.Abs_reciprocal_sqrt, bias=1.0, scale=steep[:])
+        root_v = sb.tile([P, SPLIT], F32, name="root_v")
+        root_s = sb.tile([P, I - SPLIT], F32, name="root_s")
+        for dst, src in (
+            (root_v[:, :HALF], sq[0][:]),
+            (root_v[:, HALF:], sq[1][:, : SPLIT - HALF]),
+            (root_s[:], sq[1][:, SPLIT - HALF :]),
+        ):
+            nc.scalar.activation(dst, src, ACT.Abs_reciprocal_sqrt, bias=1.0, scale=steep[:])
 
-        part0 = sb.tile([P, HALF], F32, name="part0")
-        total0 = sb.tile([P, 1], F32, name="total0")
+        part_v = sb.tile([P, SPLIT], F32, name="part_v")
+        total_v = sb.tile([P, 1], F32, name="total_v")
         nc.vector.scalar_tensor_tensor(
-            part0[:], root[0][:], 1.0, root[0][:], ALU.mult, ALU.mult, accum_out=total0[:]
+            part_v[:], root_v[:], 1.0, root_v[:], ALU.mult, ALU.mult, accum_out=total_v[:]
         )
-        part1 = sb.tile([P, HALF], F32, name="part1")
-        total1 = sb.tile([P, 1], F32, name="total1")
-        nc.scalar.activation(part1[:], root[1][:], ACT.Square, scale=root_count[:], accum_out=total1[:])
+        part_s = sb.tile([P, I - SPLIT], F32, name="part_s")
+        total_s = sb.tile([P, 1], F32, name="total_s")
+        nc.scalar.activation(part_s[:], root_s[:], ACT.Square, scale=root_count[:], accum_out=total_s[:])
         gain = sb.tile([P, 1], F32, name="gain")
-        nc.scalar.activation(gain[:], total0[:], ACT.Abs_reciprocal_sqrt, bias=total1[:], scale=1.0 / 512.0)
+        nc.scalar.activation(gain[:], total_v[:], ACT.Abs_reciprocal_sqrt, bias=total_s[:], scale=1.0 / 512.0)
         ws = sb.tile([P, I], F32, name="ws")
-        nc.vector.tensor_scalar(ws[:, halves[0]], part0[:], gain[:], gain[:], ALU.mult, ALU.mult)
-        nc.scalar.activation(ws[:, halves[1]], root[1][:], ACT.Square, scale=gain[:])
+        nc.vector.tensor_scalar(ws[:, :SPLIT], part_v[:], gain[:], gain[:], ALU.mult, ALU.mult)
+        nc.scalar.activation(ws[:, SPLIT:], root_s[:], ACT.Square, scale=gain[:])
         nc.vector.tensor_copy(placed[:].indirect(list1[:]), ws[:])
 
         for c in range(len(OUT_EDGES) - 1):

@@ -38,15 +38,18 @@ def tile_attend_exchanged_typical_counts_heads_kernel(
 
         raw_a = sb.tile([P, PACK, Q], F32, name="raw_a", tag="stage")
         nc.sync.dma_start(out=raw_a[:], in_=query.rearrange("(p j) q -> p j q", j=PACK))
+        key_words = [
+            sb.tile([P, T], U8, name="key_words_%d" % h, align_bytes=64) for h in range(2)
+        ]
+        nc.sync.dma_start(out=key_words[0][:].bitcast(I32), in_=keys_words[0, :, :T].bitcast(I32))
         for quad in range(4):
             nc.sync.dma_start(
                 out=key_scale[32 * quad : 32 * quad + 4, :].bitcast(I32),
                 in_=keys_scales[0, 4 * quad : 4 * quad + 4, :].bitcast(I32),
             )
-        key_words = sb.tile([P, 2 * T], U8, name="key_words", align_bytes=64)
-        nc.sync.dma_start(out=key_words[:].bitcast(I32), in_=keys_words[0].bitcast(I32))
         raw_b = sb.tile([P, PACK, Q], F32, name="raw_b")
         nc.sync.dma_start(out=raw_b[:], in_=query2.rearrange("(p j) q -> p j q", j=PACK))
+        nc.sync.dma_start(out=key_words[1][:].bitcast(I32), in_=keys_words[0, :, T:].bitcast(I32))
 
         list1 = lists.tile([P, I // 16], U16, name="list1")
         nc.sync.dma_start(list1[:], offs)
@@ -77,7 +80,10 @@ def tile_attend_exchanged_typical_counts_heads_kernel(
             scale = sb.tile([P, Q], U8, name="scale_" + name, align_bytes=64)
             rows = [slice(0, Q // 2), slice(Q // 2, Q)]
             for h in range(2):
-                nc.vector.tensor_copy(out=grouped[h][:], in_=raw[:, :, rows[h]].rearrange("p j q -> p q j"))
+                nc.vector.tensor_copy(
+                    out=grouped[h][:].rearrange("p (c i) j -> p c j i", i=4),
+                    in_=raw[:, :, rows[h]].rearrange("p j (c i) -> p c j i", i=4),
+                )
             for h in range(2):
                 nc.vector.quantize_mx(
                     out=codes[:, rows[h]].bitcast(FP8X4),
@@ -91,7 +97,7 @@ def tile_attend_exchanged_typical_counts_heads_kernel(
                     out=bank[:],
                     lhsT=codes[:].bitcast(FP8X4),
                     lhsT_scale=scale[:],
-                    rhs=key_words[:, 2 * n0 : 2 * (n0 + N_PASS)].bitcast(FP4X4),
+                    rhs=key_words[2 * n0 // T][:, 2 * n0 % T : 2 * n0 % T + 2 * N_PASS].bitcast(FP4X4),
                     rhs_scale=key_scale[:, n0 : n0 + N_PASS],
                     start=True,
                     stop=True,

from contextlib import ExitStack

import concourse.mybir as mybir

D, T, I, Q = 512, 1024, 512, 128
FLOPS = 2 * 2 * D * T * Q

F32 = mybir.dt.float32
BF16 = mybir.dt.bfloat16
I32 = mybir.dt.int32
U32 = mybir.dt.uint32
U16 = mybir.dt.uint16
U8 = mybir.dt.uint8
FP8X4 = mybir.dt.float8_e4m3fn_x4
FP4X4 = mybir.dt.float4_e2m1fn_x4
ALU = mybir.AluOpType
ACT = mybir.ActivationFunctionType

P = 128
PACK = 4
N_PASS = 256
HALF = I // 2
SPLIT = 320
OUT_EDGES = (0, 128, 384, 640, 896, 1024)


def tile_attend_exchanged_typical_counts_heads_kernel(
    tc, query, query2, keys_words, keys_scales, lam, width, old, fade, offs, offs2, out
):
    nc = tc.nc
    with ExitStack() as ctx:
        lists = ctx.enter_context(tc.tile_pool(name="lists", bufs=1))
        sb = ctx.enter_context(tc.tile_pool(name="sb", bufs=1))
        psum = ctx.enter_context(tc.psum_pool(name="psum", bufs=1))

        key_scale = sb.tile([P, T], U8, name="key_scale", align_bytes=64)
        nc.gpsimd.memset(key_scale[:].bitcast(I32), 0)

        raw_a = sb.tile([P, PACK, Q], F32, name="raw_a", tag="stage")
        nc.sync.dma_start(out=raw_a[:], in_=query.rearrange("(p j) q -> p j q", j=PACK))
        key_words = [
            sb.tile([P, T], U8, name="key_words_%d" % h, align_bytes=64) for h in range(2)
        ]
        nc.sync.dma_start(out=key_words[0][:].bitcast(I32), in_=keys_words[0, :, :T].bitcast(I32))
        for quad in range(4):
            nc.sync.dma_start(
                out=key_scale[32 * quad : 32 * quad + 4, :].bitcast(I32),
                in_=keys_scales[0, 4 * quad : 4 * quad + 4, :].bitcast(I32),
            )
        raw_b = sb.tile([P, PACK, Q], F32, name="raw_b")
        nc.sync.dma_start(out=raw_b[:], in_=query2.rearrange("(p j) q -> p j q", j=PACK))
        nc.sync.dma_start(out=key_words[1][:].bitcast(I32), in_=keys_words[0, :, T:].bitcast(I32))

        list1 = lists.tile([P, I // 16], U16, name="list1")
        nc.sync.dma_start(list1[:], offs)
        list2 = lists.tile([P, I // 16], U16, name="list2")
        nc.sync.dma_start(list2[:], offs2)

        width_col = sb.tile([P, 1], F32, name="width_col")
        nc.sync.dma_start(out=width_col[:], in_=width)
        lam_col = sb.tile([P, 1], F32, name="lam_col")
        nc.sync.dma_start(out=lam_col[:], in_=lam)
        fade_col = sb.tile([P, 1], F32, name="fade_col")
        nc.sync.dma_start(out=fade_col[:], in_=fade)

        placed = sb.tile([P, T], F32, name="placed")
        nc.vector.memset(placed[:], 0.0)

        count = sb.tile([P, 1], F32, name="count")
        nc.vector.memset(count[:], 512.0)
        root_count = sb.tile([P, 1], F32, name="root_count")
        nc.scalar.activation(root_count[:], count[:], ACT.Abs_reciprocal_sqrt)

        scores = []
        for name, raw in (("a", raw_a), ("b", raw_b)):
            grouped = [
                sb.tile([P, Q // 2, PACK], BF16, name="grouped_%s%d" % (name, h), align_bytes=64) for h in range(2)
            ]
            codes = sb.tile([P, Q], U32, name="codes_" + name, align_bytes=64)
            scale = sb.tile([P, Q], U8, name="scale_" + name, align_bytes=64)
            rows = [slice(0, Q // 2), slice(Q // 2, Q)]
            for h in range(2):
                nc.vector.tensor_copy(
                    out=grouped[h][:].rearrange("p (c i) j -> p c j i", i=4),
                    in_=raw[:, :, rows[h]].rearrange("p j (c i) -> p c j i", i=4),
                )
            for h in range(2):
                nc.vector.quantize_mx(
                    out=codes[:, rows[h]].bitcast(FP8X4),
                    scales=scale[:, rows[h]],
                    in_=grouped[h][:].rearrange("p q j -> p (q j)"),
                )
            whole = sb.tile([P, T], F32, name="whole_" + name, tag="whole_" + name)
            for n0 in range(0, T, N_PASS):
                bank = psum.tile([P, N_PASS], F32, name="bank_%s%d" % (name, n0))
                nc.tensor.matmul_mx(
                    out=bank[:],
                    lhsT=codes[:].bitcast(FP8X4),
                    lhsT_scale=scale[:],
                    rhs=key_words[2 * n0 // T][:, 2 * n0 % T : 2 * n0 % T + 2 * N_PASS].bitcast(FP4X4),
                    rhs_scale=key_scale[:, n0 : n0 + N_PASS],
                    start=True,
                    stop=True,
                )
                nc.scalar.activation(whole[:, n0 : n0 + N_PASS], bank[:], ACT.Copy)
            scores.append(whole)
        a_all, b_all = scores

        old_rows = sb.tile([P, T], F32, name="old_rows", tag="stage")
        nc.sync.dma_start(out=old_rows[:], in_=old)

        halves = [slice(0, HALF), slice(HALF, I)]
        cols = [slice(0, HALF // 16), slice(HALF // 16, I // 16)]
        a1 = sb.tile([P, I], F32, name="a1")
        a2 = sb.tile([P, I], F32, name="a2")
        nc.vector.tensor_copy(a1[:], a_all[:].indirect(list1[:]))
        nc.vector.tensor_copy(a2[:], a_all[:].indirect(list2[:]))
        b1 = [sb.tile([P, HALF], F32, name="b1_%d" % h) for h in range(2)]
        b2 = [sb.tile([P, HALF], F32, name="b2_%d" % h) for h in range(2)]
        for h in range(2):
            nc.scalar.activation(b2[h][:], b_all[:].indirect(list2[:, cols[h]]), ACT.Copy)
            nc.scalar.activation(b1[h][:], b_all[:].indirect(list1[:, cols[h]]), ACT.Copy)

        wide_sq = sb.tile([P, 1], F32, name="wide_sq", tag="whole_b")
        nc.scalar.activation(wide_sq[:], width_col[:], ACT.Square, scale=float(I))
        inv_wide = sb.tile([P, 1], F32, name="inv_wide")
        nc.scalar.activation(inv_wide[:], wide_sq[:], ACT.Abs_reciprocal_sqrt)
        steep = sb.tile([P, 1], F32, name="steep")
        nc.scalar.activation(steep[:], inv_wide[:], ACT.Square, scale=lam_col[:])

        first = [sb.tile([P, HALF], F32, name="first_%d" % h) for h in range(2)]
        second = [sb.tile([P, HALF], F32, name="second_%d" % h) for h in range(2)]
        diff = [sb.tile([P, HALF], F32, name="diff_%d" % h) for h in range(2)]
        sum_first = [sb.tile([P, 1], F32, name="sum_first_%d" % h) for h in range(2)]
        sum_second = [sb.tile([P, 1], F32, name="sum_second_%d" % h) for h in range(2)]
        sum_diff0 = sb.tile([P, 1], F32, name="sum_diff0")
        for h in range(2):
            nc.vector.scalar_tensor_tensor(
                first[h][:], a1[:, halves[h]], 1.0, b2[h][:], ALU.mult, ALU.max, accum_out=sum_first[h][:]
            )
            if h == 1:
                nc.vector.tensor_tensor(sum_diff0[:], sum_first[0][:], sum_second[0][:], ALU.subtract)
            nc.vector.scalar_tensor_tensor(
                second[h][:], a2[:, halves[h]], 1.0, b1[h][:], ALU.mult, ALU.max, accum_out=sum_second[h][:]
            )
        nc.vector.tensor_tensor(diff[0][:], first[0][:], second[0][:], ALU.subtract)
        minus_sum = sb.tile([P, 1], F32, name="minus_sum")
        nc.vector.tensor_scalar(
            minus_sum[:], sum_second[1][:], sum_diff0[:], sum_first[1][:], ALU.subtract, ALU.subtract
        )
        nc.vector.tensor_tensor(diff[1][:], first[1][:], second[1][:], ALU.subtract)

        sq = [sb.tile([P, HALF], F32, name="sq_%d" % h) for h in range(2)]
        for h in range(2):
            nc.scalar.activation(sq[h][:], diff[h][:], ACT.Square, bias=minus_sum[:], scale=float(I))
        root_v = sb.tile([P, SPLIT], F32, name="root_v")
        root_s = sb.tile([P, I - SPLIT], F32, name="root_s")
        for dst, src in (
            (root_v[:, :HALF], sq[0][:]),
            (root_v[:, HALF:], sq[1][:, : SPLIT - HALF]),
            (root_s[:], sq[1][:, SPLIT - HALF :]),
        ):
            nc.scalar.activation(dst, src, ACT.Abs_reciprocal_sqrt, bias=1.0, scale=steep[:])

        part_v = sb.tile([P, SPLIT], F32, name="part_v")
        total_v = sb.tile([P, 1], F32, name="total_v")
        nc.vector.scalar_tensor_tensor(
            part_v[:], root_v[:], 1.0, root_v[:], ALU.mult, ALU.mult, accum_out=total_v[:]
        )
        part_s = sb.tile([P, I - SPLIT], F32, name="part_s")
        total_s = sb.tile([P, 1], F32, name="total_s")
        nc.scalar.activation(part_s[:], root_s[:], ACT.Square, scale=root_count[:], accum_out=total_s[:])
        gain = sb.tile([P, 1], F32, name="gain")
        nc.scalar.activation(gain[:], total_v[:], ACT.Abs_reciprocal_sqrt, bias=total_s[:], scale=1.0 / 512.0)
        ws = sb.tile([P, I], F32, name="ws")
        nc.vector.tensor_scalar(ws[:, :SPLIT], part_v[:], gain[:], gain[:], ALU.mult, ALU.mult)
        nc.scalar.activation(ws[:, SPLIT:], root_s[:], ACT.Square, scale=gain[:])
        nc.vector.tensor_copy(placed[:].indirect(list1[:]), ws[:])

        for c in range(len(OUT_EDGES) - 1):
            span = slice(OUT_EDGES[c], OUT_EDGES[c + 1])
            result = sb.tile([P, span.stop - span.start], F32, name="result_%d" % c)
            nc.vector.scalar_tensor_tensor(
                result[:], old_rows[:, span], fade_col[:], placed[:, span], ALU.mult, ALU.add
            )
            queue = nc.sync if c % 2 == 0 else nc.scalar
            queue.dma_start(out=out[:, span], in_=result[:])
